import numpy as np
import ml_dtypes


def mxq(x, axis, fmt="e4m3"):
    dtype, down = {"e4m3": (ml_dtypes.float8_e4m3fn, 7), "e5m2": (ml_dtypes.float8_e5m2, 14)}[fmt]
    v = np.moveaxis(np.asarray(x, np.float32).astype(ml_dtypes.bfloat16).astype(np.float64), axis, -1)
    blocks = v.reshape(v.shape[:-1] + (-1, 32))
    amax = np.abs(blocks).max(-1, keepdims=True)
    byte = np.maximum(np.where(amax > 0, np.frexp(amax)[1] - 1 + 127, 0) - down, 1)
    scale = np.exp2(byte - 127.0)
    codes = (blocks / scale).astype(np.float32).astype(dtype).astype(np.float64)
    return np.moveaxis((codes * scale).reshape(v.shape), -1, axis)


WIDE = False


def mx_kscale(k):
    if not WIDE:
        return np.ones(k)
    levels = np.array([10, -10, 5, -5, 0])
    if k % 512:
        return np.exp2(np.random.permutation(np.resize(levels, k // 32))).repeat(32)
    a = np.empty((k // 512, 16))
    for p in range(k // 512):
        a[p, :8] = np.random.permutation(np.resize(levels, 8))
        for g in range(8):
            far = levels[np.abs(levels - a[p, g]) >= 10]
            a[p, g + 8] = far[np.random.randint(len(far))]
    return np.exp2(a.ravel()).repeat(32)


def f64(x):
    return np.asarray(x).astype(np.float64)


def striped(idx):
    return np.tile(idx.reshape(-1, 16).T, (8, 1)).astype(np.uint16)


def unstriped(offs):
    return offs[:16].T.reshape(-1).astype(np.int64)


E2M1 = np.array([0.0, 0.5, 1.0, 1.5, 2.0, 3.0, 4.0, 6.0, -0.0, -0.5, -1.0, -1.5, -2.0, -3.0, -4.0, -6.0])


def pack_weight(w, fmt):
    k, n = w.shape
    w = f64(np.asarray(w, np.float32).astype(ml_dtypes.bfloat16)).reshape(k // 32, 32, n)
    amax = np.abs(w).max(1)
    if fmt == "e4m3":
        byte = np.frexp(amax)[1] - 1 + 127 - 7
    else:
        mant, ex = np.frexp(amax / 6.0)
        byte = np.where(mant > 0.5, ex, ex - 1) + 127
    byte = np.clip(np.where(amax > 0, byte, 1), 1, 254)
    scaled = (w * np.exp2(127.0 - byte)[:, None, :]).reshape(k, n).astype(np.float32)
    by_word = np.ascontiguousarray(scaled.reshape(k // 512, 128, 4, n).transpose(0, 1, 3, 2))
    if fmt == "e4m3":
        words = by_word.astype(ml_dtypes.float8_e4m3fn).view(np.uint8)
    else:
        c = by_word.astype(ml_dtypes.float4_e2m1fn).view(np.uint8) & 0xF
        words = (c[..., 0::2] | (c[..., 1::2] << 4)).reshape(k // 512, 128, 2 * n)
    return np.ascontiguousarray(words), np.ascontiguousarray(byte.astype(np.uint8).reshape(k // 512, 16, n))


def unpack_weight(words, scales, fmt):
    g, _, n = scales.shape
    words = np.ascontiguousarray(words).reshape(g, 128, n, -1)
    if fmt == "e4m3":
        vals = words.view(ml_dtypes.float8_e4m3fn).astype(np.float64)
    else:
        nib = np.empty((g, 128, n, 4), np.uint8)
        nib[..., 0::2] = words & 0xF
        nib[..., 1::2] = words >> 4
        vals = E2M1[nib]
    vals = vals * np.repeat(np.exp2(scales.astype(np.float64) - 127.0), 8, axis=1)[..., None]
    return vals.transpose(0, 1, 3, 2).reshape(g * 512, n)


def gelu(v):
    return 0.5 * v * (1.0 + np.tanh(np.sqrt(2.0 / np.pi) * (v + 0.044715 * v**3)))


K, H, N, T, S, P = 1536, 1024, 768, 4096, 1024, 512

def setup_inputs():
    n = np.random.standard_normal
    s = mx_kscale(K)[:, None]
    u = mx_kscale(H)[:, None]
    tab_words, tab_scales = pack_weight(n((K, T)) * s, "e4m3")
    w4_words, w4_scales = pack_weight(n((H, N)) / np.sqrt(H) / u, "e2m1")
    sign = np.random.choice([-1.0, 1.0], H)
    perm = np.random.permutation(S)
    return {
        "tab_words": tab_words, "tab_scales": tab_scales,
        "offs": striped(np.random.permutation(T)[:S]),
        "pos1": striped(perm[:P]),
        "pos2": striped(perm[P:]),
        "w1": (0.9 * n((K, H)) / np.sqrt(K) / s).astype(np.float32),
        "b1": (0.4 * n(H)).astype(np.float32),
        "thr": n(H).astype(np.float32),
        "base": (0.4 * n(H)).astype(np.float32),
        "wgs": np.exp(0.3 * n((128, P))).astype(np.float32),
        "gain": (sign * np.random.uniform(0.6, 1.6, H) * u[:, 0]).astype(np.float32),
        "w4_words": w4_words, "w4_scales": w4_scales,
        "res": (0.4 * n((N, S))).astype(np.float32),
    }

def reference(tab_words, tab_scales, offs, pos1, pos2, w1, b1, thr, base, wgs, gain, w4_words, w4_scales, res):
    v = unpack_weight(tab_words, tab_scales, "e4m3")[:, unstriped(offs)]
    w1q = mxq(f64(w1), 0, "e4m3")
    h = (w1q.T @ v) + f64(b1)[:, None]
    a = 1.0 / (1.0 + np.exp(-(h[:, unstriped(pos1)] + f64(thr)[:, None])))
    page = np.maximum(h, f64(base)[:, None])
    page[:, unstriped(pos2)] = np.tile(f64(wgs), (H // 128, 1)) * a
    z = mxq(f64(gain)[:, None] * page, 0, "e4m3")
    w4 = unpack_weight(w4_words, w4_scales, "e2m1")
    return (w4.T @ z) + f64(res)

@@ -1,0 +1,273 @@
+from contextlib import ExitStack
+
+import concourse.mybir as mybir
+
+K, H, N, T, S, M = 1536, 1024, 768, 4096, 1024, 512
+FLOPS = 2 * K * H * S + 2 * H * N * S
+
+F32 = mybir.dt.float32
+BF16 = mybir.dt.bfloat16
+I32 = mybir.dt.int32
+U32 = mybir.dt.uint32
+U16 = mybir.dt.uint16
+U8 = mybir.dt.uint8
+FP8X4 = mybir.dt.float8_e4m3fn_x4
+FP4X4 = mybir.dt.float4_e2m1fn_x4
+ACT = mybir.ActivationFunctionType
+ALU = mybir.AluOpType
+
+P = 128
+PACK = 4
+PASS = P * PACK
+BANK = 512
+KP = K // PASS
+HP = H // PASS
+HALVES = S // BANK
+NT = N // P
+ROWSETS = HP * PACK
+
+
+def tile_list_washed_stroke_fill_kernel(
+    tc, tab_words, tab_scales, offs, pos1, pos2, w1, b1, thr, base, wgs, gain, w4_words, w4_scales, res, out
+):
+    nc = tc.nc
+    with ExitStack() as ctx:
+        lists = ctx.enter_context(tc.tile_pool(name="lists", bufs=1))
+        keep = ctx.enter_context(tc.tile_pool(name="keep", bufs=1))
+        ring = ctx.enter_context(tc.tile_pool(name="ring", bufs=1))
+        psum = ctx.enter_context(tc.psum_pool(name="psum", bufs=1))
+
+        offs_sb = lists.tile([P, S // 16], U16, name="offs_sb")
+        pos1_sb = lists.tile([P, M // 16], U16, name="pos1_sb")
+        pos2_sb = lists.tile([P, M // 16], U16, name="pos2_sb")
+
+        tab_sc = keep.tile([P, T], U8, name="tab_sc", align_bytes=64)
+        nc.vector.memset(tab_sc[:].bitcast(I32), 0)
+        for q in range(4):
+            nc.scalar.dma_start(
+                out=tab_sc[32 * q : 32 * q + 4 * KP, :].bitcast(I32),
+                in_=tab_scales[:, 4 * q : 4 * q + 4, :].bitcast(I32),
+            )
+        rowvec = {}
+        w4_sc = keep.tile([P, HP, N], U8, name="w4_sc", align_bytes=64)
+        nc.vector.memset(w4_sc[:].bitcast(I32), 0)
+
+        def col(name, i):
+            return rowvec[name][:, i // PACK, i % PACK : i % PACK + 1]
+
+        tab_sb, raw = {}, {}
+
+        def load_tab(a):
+            tab_sb[a] = keep.tile([P, T], U32, name="tab%d" % a)
+            nc.sync.dma_start(
+                out=tab_sb[a][:].bitcast(I32), in_=tab_words[a].rearrange("p t i -> p (t i)").bitcast(I32)
+            )
+
+        def load_w1(b, a):
+            parts = 2 if a == KP - 1 else 1
+            width = PASS // parts
+            for u in range(parts):
+                raw[b, a, u] = ring.tile([P, PACK, width], F32, name="raw%d%d%d" % (b, a, u), tag="raw%d%d%d" % (b, a, u))
+                c0 = b * PASS + u * width
+                nc.sync.dma_start(
+                    out=raw[b, a, u][:],
+                    in_=w1[a * PASS : (a + 1) * PASS, c0 : c0 + width].rearrange("(p j) c -> p j c", j=PACK),
+                )
+
+        wgs_sb = keep.tile([P, PACK, M], F32, name="wgs_sb")
+
+        nc.sync.dma_start(offs_sb[:], offs)
+        load_tab(0)
+        load_w1(0, 0)
+        nc.sync.dma_start(pos1_sb[:], pos1)
+        nc.sync.dma_start(pos2_sb[:], pos2)
+        load_tab(1)
+        for name, vec in (("b1", b1), ("thr", thr), ("base", base), ("gain", gain)):
+            rowvec[name] = keep.tile([P, HP, PACK], F32, name="row_" + name)
+            nc.sync.dma_start(out=rowvec[name][:], in_=vec.rearrange("(b p t) -> p b t", b=HP, t=PACK))
+        load_w1(0, 1)
+        load_tab(2)
+        load_w1(0, 2)
+        for q in (0, 2, 1, 3):
+            nc.sync.dma_start(out=wgs_sb[32 * q : 32 * (q + 1), :, :], in_=wgs.rearrange("(q t) m -> q t m", t=PACK))
+        for a in range(KP):
+            load_w1(1, a)
+        w4_sb = keep.tile([P, HP, 2 * N], U8, name="w4_sb", align_bytes=64)
+        nc.sync.dma_start(out=w4_sb[:].bitcast(I32), in_=w4_words.bitcast(I32).rearrange("a p c -> p a c"))
+        for q in range(4):
+            nc.sync.dma_start(
+                out=w4_sc[32 * q : 32 * q + 4, :, :].bitcast(I32),
+                in_=w4_scales[:, 4 * q : 4 * q + 4, :].bitcast(I32).rearrange("a r n -> r a n"),
+            )
+
+        v_words = {}
+        v_sc = keep.tile([P, S], U8, name="v_sc", align_bytes=64)
+
+        def gather_words(a):
+            v_words[a] = keep.tile([P, S], U32, name="v_words%d" % a, align_bytes=64)
+            nc.vector.tensor_copy(v_words[a][:], tab_sb[a][:].indirect(offs_sb[:]))
+
+        w1_codes, w1_sc = {}, {}
+
+        def quantise_w1(b, a):
+            grouped = ring.tile([P, PACK, P, PACK], BF16, name="grouped", tag="stage%d" % ((b * KP + a) % 2), align_bytes=64)
+            parts = 2 if a == KP - 1 else 1
+            mw = P // parts
+            for u in range(parts):
+                src = raw[b, a, u][:].rearrange("p j (m t) -> p m t j", t=PACK)
+                dst = grouped[:, :, u * mw : (u + 1) * mw, :].rearrange("p t m j -> p m t j")
+                if u == 0:
+                    nc.scalar.copy(out=dst, in_=src)
+                else:
+                    nc.vector.tensor_copy(out=dst, in_=src)
+            w1_codes[b, a] = keep.tile([P, PASS], U32, name="w1c%d%d" % (b, a), align_bytes=64)
+            w1_sc[b, a] = keep.tile([P, PASS], U8, name="w1s%d%d" % (b, a), align_bytes=64)
+            flat = grouped[:].rearrange("p t m j -> p (t m j)")
+            cuts = (0, P, PASS) if a == KP - 1 else (0, PASS)
+            for c0, c1 in zip(cuts, cuts[1:]):
+                nc.vector.quantize_mx(
+                    out=w1_codes[b, a][:, c0:c1].bitcast(FP8X4),
+                    scales=w1_sc[b, a][:, c0:c1],
+                    in_=flat[:, PACK * c0 : PACK * c1],
+                )
+
+        sums = {}
+
+        def first_product(i, a):
+            b, t = divmod(i, PACK)
+            for u in range(HALVES):
+                if a == 0:
+                    sums[i, u] = psum.tile([P, BANK], F32, name="sums", tag="bank%d" % (HALVES * t + u))
+                cols = slice(u * BANK, (u + 1) * BANK)
+                nc.tensor.matmul_mx(
+                    out=sums[i, u][:],
+                    lhsT=w1_codes[b, a][:, t * P : (t + 1) * P].bitcast(FP8X4),
+                    lhsT_scale=w1_sc[b, a][:, t * P : (t + 1) * P],
+                    rhs=v_words[a][:, cols].bitcast(FP8X4),
+                    rhs_scale=v_sc[4 * a : P, cols],
+                    start=(a == 0),
+                    stop=(a == KP - 1),
+                )
+
+        page = {}
+
+        def fill_page(i):
+            tag = {1: "h0", 2: "raw100", 3: "raw120"}.get(i, "h%d" % (i % 3))
+            h = ring.tile([P, S], F32, name="h", tag=tag)
+            for u in range(HALVES):
+                cols = slice(u * BANK, (u + 1) * BANK)
+                if i == 0:
+                    nc.vector.tensor_scalar_add(out=h[:, cols], in0=sums[i, u][:], scalar1=col("b1", i))
+                else:
+                    nc.scalar.activation(out=h[:, cols], in_=sums[i, u][:], func=ACT.Identity, bias=col("b1", i))
+            look = ring.tile([P, M], F32, name="look", tag="look", bufs=4)
+            nc.scalar.activation(out=look[:], in_=h[:].indirect(pos1_sb[:]), func=ACT.Sigmoid, bias=col("thr", i))
+            page[i] = ring.tile([P, S], F32, name="page", tag="page", bufs=6)
+            nc.vector.tensor_scalar_max(out=page[i][:], in0=h[:], scalar1=col("base", i))
+            nc.vector.tensor_tensor(page[i][:].indirect(pos2_sb[:]), look[:], wgs_sb[:, i % PACK, :], ALU.mult)
+
+        planes = {}
+
+        def round_page(i):
+            b, t = divmod(i, PACK)
+            if b == 0:
+                if t == 0:
+                    whole = ring.tile([P, PACK, S], BF16, name="whole", tag="raw120")
+                    for u in range(HALVES):
+                        planes[b, u] = whole[:, :, u * BANK : (u + 1) * BANK]
+                    planes[b] = whole
+                nc.scalar.activation(out=planes[b][:, t, :], in_=page[i][:], func=ACT.Copy, scale=col("gain", i))
+                return
+            for u in range(HALVES):
+                if t == 0:
+                    planes[b, u] = ring.tile([P, PACK, BANK], BF16, name="planes", tag="planes%d" % u)
+                nc.scalar.activation(
+                    out=planes[b, u][:, t, :], in_=page[i][:, u * BANK : (u + 1) * BANK], func=ACT.Copy, scale=col("gain", i)
+                )
+
+        z_codes, z_sc = {}, {}
+
+        def quantise_z(b, u):
+            woven = ring.tile([P, BANK, PACK], BF16, name="woven", tag="woven%d" % u, align_bytes=64)
+            dst = woven[:].rearrange("p (c i) t -> p c t i", i=4)
+            src = planes[b, u][:, :, :].rearrange("p t (c i) -> p c t i", i=4)
+            if b == HP - 1 and u == HALVES - 1:
+                nc.scalar.copy(out=dst, in_=src)
+            else:
+                nc.vector.tensor_copy(out=dst, in_=src)
+            z_codes[b, u] = keep.tile([P, BANK], U32, name="zc%d%d" % (b, u), align_bytes=64)
+            z_sc[b, u] = keep.tile([P, BANK], U8, name="zs%d%d" % (b, u), align_bytes=64)
+            nc.vector.quantize_mx(
+                out=z_codes[b, u][:].bitcast(FP8X4), scales=z_sc[b, u][:], in_=woven[:].rearrange("p c t -> p (c t)")
+            )
+
+        groups = [(u, n) for u in range(HALVES) for n in range(NT)]
+        outs = {}
+
+        def second_product(g, b):
+            u, n = groups[g]
+            if b == 0:
+                outs[g] = psum.tile([P, BANK], F32, name="outs", tag="bank%d" % (g % 8))
+            nc.tensor.matmul_mx(
+                out=outs[g][:],
+                lhsT=w4_sb[:, b, 2 * P * n : 2 * P * (n + 1)].bitcast(FP4X4),
+                lhsT_scale=w4_sc[:, b, P * n : P * (n + 1)],
+                rhs=z_codes[b, u][:].bitcast(FP8X4),
+                rhs_scale=z_sc[b, u][:],
+                start=(b == 0),
+                stop=(b == HP - 1),
+            )
+
+        gather_words(0)
+        quantise_w1(0, 0)
+        nc.vector.tensor_copy(v_sc[:], tab_sc[:].indirect(offs_sb[:]))
+        for a in range(KP):
+            if a > 0:
+                gather_words(a)
+                quantise_w1(0, a)
+            for t in range(PACK):
+                first_product(t, a)
+
+        res_sb = {}
+        for k in range(NT // 2):
+            tag = "raw0%d0" % k if k < 2 else "res_last"
+            res_sb[k] = ring.tile([P, 2, S], F32, name="res_sb", tag=tag)
+            nc.sync.dma_start(
+                out=res_sb[k][:], in_=res[2 * P * k : 2 * P * (k + 1), :].rearrange("(e p) j -> p e j", p=P)
+            )
+
+        fill_page(0)
+        fill_page(1)
+        quantise_w1(1, 0)
+        fill_page(2)
+        quantise_w1(1, 1)
+        quantise_w1(1, 2)
+        fill_page(3)
+        for t in range(PACK):
+            for a in range(KP):
+                first_product(PACK + t, a)
+        fill_page(4)
+        fill_page(5)
+        round_page(0)
+        round_page(1)
+        fill_page(6)
+        round_page(2)
+        round_page(3)
+        fill_page(7)
+        for u in range(HALVES):
+            quantise_z(0, u)
+        for g in range(8):
+            second_product(g, 0)
+        for i in range(PACK, ROWSETS):
+            round_page(i)
+
+        for u in range(HALVES):
+            quantise_z(1, u)
+        for g in range(len(groups)):
+            u, n = groups[g]
+            if g >= 8:
+                second_product(g, 0)
+            second_product(g, 1)
+            dst = res_sb[n // 2][:, n % 2, u * BANK : (u + 1) * BANK]
+            nc.vector.tensor_tensor(out=dst, in0=outs[g][:], in1=dst, op=ALU.add)
+            nc.sync.dma_start(out=out[n * P : (n + 1) * P, u * BANK : (u + 1) * BANK], in_=dst)

@@ -1,6 +1,7 @@
 from contextlib import ExitStack
 
 import concourse.mybir as mybir
+from concourse.masks import make_identity
 
 K, H, N, T, S, M = 1536, 1024, 768, 4096, 1024, 512
 FLOPS = 2 * K * H * S + 2 * H * N * S
@@ -41,10 +42,12 @@ def tile_list_washed_stroke_fill_kernel(
         pos1_sb = lists.tile([P, M // 16], U16, name="pos1_sb")
         pos2_sb = lists.tile([P, M // 16], U16, name="pos2_sb")
 
-        tab_sc = keep.tile([P, T], U8, name="tab_sc", align_bytes=64)
+        ident = keep.tile([P, P], F32, name="ident")
+        make_identity(nc, ident[:])
+        tab_sc = ring.tile([P, T], U8, name="tab_sc", tag="tab_sc", align_bytes=64)
         nc.vector.memset(tab_sc[:].bitcast(I32), 0)
         for q in range(4):
-            nc.scalar.dma_start(
+            nc.gpsimd.dma_start(
                 out=tab_sc[32 * q : 32 * q + 4 * KP, :].bitcast(I32),
                 in_=tab_scales[:, 4 * q : 4 * q + 4, :].bitcast(I32),
             )
@@ -77,6 +80,8 @@ def tile_list_washed_stroke_fill_kernel(
         wgs_sb = keep.tile([P, PACK, M], F32, name="wgs_sb")
 
         nc.sync.dma_start(offs_sb[:], offs)
+        wgs_rows = ring.tile([P, M], F32, name="wgs_rows", tag="look", bufs=4)
+        nc.sync.dma_start(out=wgs_rows[:], in_=wgs)
         load_tab(0)
         load_w1(0, 0)
         nc.sync.dma_start(pos1_sb[:], pos1)
@@ -88,8 +93,6 @@ def tile_list_washed_stroke_fill_kernel(
         load_w1(0, 1)
         load_tab(2)
         load_w1(0, 2)
-        for q in (0, 2, 1, 3):
-            nc.sync.dma_start(out=wgs_sb[32 * q : 32 * (q + 1), :, :], in_=wgs.rearrange("(q t) m -> q t m", t=PACK))
         for a in range(KP):
             load_w1(1, a)
         w4_sb = keep.tile([P, HP, 2 * N], U8, name="w4_sb", align_bytes=64)
@@ -110,13 +113,14 @@ def tile_list_washed_stroke_fill_kernel(
         w1_codes, w1_sc = {}, {}
 
         def quantise_w1(b, a):
-            grouped = ring.tile([P, PACK, P, PACK], BF16, name="grouped", tag="stage%d" % ((b * KP + a) % 2), align_bytes=64)
+            tag = "tab_sc" if a == 1 else "stage%d" % (a // 2)
+            grouped = ring.tile([P, PACK, P, PACK], BF16, name="grouped", tag=tag, align_bytes=64)
             parts = 2 if a == KP - 1 else 1
             mw = P // parts
             for u in range(parts):
                 src = raw[b, a, u][:].rearrange("p j (m t) -> p m t j", t=PACK)
                 dst = grouped[:, :, u * mw : (u + 1) * mw, :].rearrange("p t m j -> p m t j")
-                if u == 0:
+                if u == 0 and (b, a) != (1, 0):
                     nc.scalar.copy(out=dst, in_=src)
                 else:
                     nc.vector.tensor_copy(out=dst, in_=src)
@@ -149,10 +153,10 @@ def tile_list_washed_stroke_fill_kernel(
                     stop=(a == KP - 1),
                 )
 
-        page = {}
+        page, hs = {}, {}
 
-        def fill_page(i):
-            tag = {1: "h0", 2: "raw100", 3: "raw120"}.get(i, "h%d" % (i % 3))
+        def lay_page(i):
+            tag = {1: "h0", 2: "raw120"}.get(i, "h%d" % (i % 3))
             h = ring.tile([P, S], F32, name="h", tag=tag)
             for u in range(HALVES):
                 cols = slice(u * BANK, (u + 1) * BANK)
@@ -160,11 +164,21 @@ def tile_list_washed_stroke_fill_kernel(
                     nc.vector.tensor_scalar_add(out=h[:, cols], in0=sums[i, u][:], scalar1=col("b1", i))
                 else:
                     nc.scalar.activation(out=h[:, cols], in_=sums[i, u][:], func=ACT.Identity, bias=col("b1", i))
-            look = ring.tile([P, M], F32, name="look", tag="look", bufs=4)
-            nc.scalar.activation(out=look[:], in_=h[:].indirect(pos1_sb[:]), func=ACT.Sigmoid, bias=col("thr", i))
             page[i] = ring.tile([P, S], F32, name="page", tag="page", bufs=6)
             nc.vector.tensor_scalar_max(out=page[i][:], in0=h[:], scalar1=col("base", i))
-            nc.vector.tensor_tensor(page[i][:].indirect(pos2_sb[:]), look[:], wgs_sb[:, i % PACK, :], ALU.mult)
+            hs[i] = h
+
+        def put_looks(i):
+            h = hs[i]
+            look = ring.tile([P, M], F32, name="look", tag="look", bufs=4)
+            parts = 2 if i == 0 else 1
+            for e in range(parts):
+                ent = slice(e * M // parts, (e + 1) * M // parts)
+                lst = slice(e * M // parts // 16, (e + 1) * M // parts // 16)
+                nc.scalar.activation(
+                    out=look[:, ent], in_=h[:].indirect(pos1_sb[:, lst]), func=ACT.Sigmoid, bias=col("thr", i)
+                )
+                nc.vector.tensor_tensor(page[i][:].indirect(pos2_sb[:, lst]), look[:, ent], wgs_sb[:, i % PACK, ent], ALU.mult)
 
         planes = {}
 
@@ -189,17 +203,23 @@ def tile_list_washed_stroke_fill_kernel(
 
         def quantise_z(b, u):
             woven = ring.tile([P, BANK, PACK], BF16, name="woven", tag="woven%d" % u, align_bytes=64)
-            dst = woven[:].rearrange("p (c i) t -> p c t i", i=4)
-            src = planes[b, u][:, :, :].rearrange("p t (c i) -> p c t i", i=4)
-            if b == HP - 1 and u == HALVES - 1:
-                nc.scalar.copy(out=dst, in_=src)
-            else:
-                nc.vector.tensor_copy(out=dst, in_=src)
             z_codes[b, u] = keep.tile([P, BANK], U32, name="zc%d%d" % (b, u), align_bytes=64)
             z_sc[b, u] = keep.tile([P, BANK], U8, name="zs%d%d" % (b, u), align_bytes=64)
-            nc.vector.quantize_mx(
-                out=z_codes[b, u][:].bitcast(FP8X4), scales=z_sc[b, u][:], in_=woven[:].rearrange("p c t -> p (c t)")
-            )
+            urgent = (b, u) == (HP - 1, 0)
+            pieces = [slice(0, BANK // 2), slice(BANK // 2, BANK)] if urgent else [slice(0, BANK)]
+            for cols in pieces:
+                dst = woven[:, cols, :].rearrange("p (c i) t -> p c t i", i=4)
+                src = planes[b, u][:, :, cols].rearrange("p t (c i) -> p c t i", i=4)
+                if urgent:
+                    nc.vector.tensor_copy(out=dst, in_=src)
+                else:
+                    nc.scalar.copy(out=dst, in_=src)
+            for cols in pieces:
+                nc.vector.quantize_mx(
+                    out=z_codes[b, u][:, cols].bitcast(FP8X4),
+                    scales=z_sc[b, u][:, cols],
+                    in_=woven[:, cols, :].rearrange("p c t -> p (c t)"),
+                )
 
         groups = [(u, n) for u in range(HALVES) for n in range(NT)]
         outs = {}
@@ -208,15 +228,29 @@ def tile_list_washed_stroke_fill_kernel(
             u, n = groups[g]
             if b == 0:
                 outs[g] = psum.tile([P, BANK], F32, name="outs", tag="bank%d" % (g % 8))
-            nc.tensor.matmul_mx(
-                out=outs[g][:],
-                lhsT=w4_sb[:, b, 2 * P * n : 2 * P * (n + 1)].bitcast(FP4X4),
-                lhsT_scale=w4_sc[:, b, P * n : P * (n + 1)],
-                rhs=z_codes[b, u][:].bitcast(FP8X4),
-                rhs_scale=z_sc[b, u][:],
-                start=(b == 0),
-                stop=(b == HP - 1),
-            )
+            pieces = [slice(0, BANK // 2), slice(BANK // 2, BANK)] if (g, b) == (0, HP - 1) else [slice(0, BANK)]
+            for cols in pieces:
+                nc.tensor.matmul_mx(
+                    out=outs[g][:, cols],
+                    lhsT=w4_sb[:, b, 2 * P * n : 2 * P * (n + 1)].bitcast(FP4X4),
+                    lhsT_scale=w4_sc[:, b, P * n : P * (n + 1)],
+                    rhs=z_codes[b, u][:, cols].bitcast(FP8X4),
+                    rhs_scale=z_sc[b, u][:, cols],
+                    start=(b == 0),
+                    stop=(b == HP - 1 and cols.stop == BANK),
+                )
+
+        turned = psum.tile([P, M // P, P], F32, name="turned", tag="bank0")
+        for k in range(M // P):
+            nc.tensor.transpose(turned[:, k, :], wgs_rows[:, k * P : (k + 1) * P], ident[:])
+        dealt = ring.tile([P, M // P, PACK, P], F32, name="dealt", tag="dealt")
+        for c in range(4):
+            nc.vector.tensor_copy(out=dealt[:, :, :, 32 * c : 32 * (c + 1)], in_=turned[:].rearrange("m k (q t) -> m k t q", t=PACK))
+        for t in range(PACK):
+            back = psum.tile([P, M // P, P], F32, name="back", tag="bank%d" % (1 + t))
+            for k in range(M // P):
+                nc.tensor.transpose(back[:, k, :], dealt[:, k, t, :], ident[:])
+            nc.scalar.copy(out=wgs_sb[:, t, :], in_=back[:].rearrange("p k m -> p (k m)"))
 
         gather_words(0)
         quantise_w1(0, 0)
@@ -230,32 +264,38 @@ def tile_list_washed_stroke_fill_kernel(
 
         res_sb = {}
         for k in range(NT // 2):
-            tag = "raw0%d0" % k if k < 2 else "res_last"
+            tag = "raw0%d0" % k if k < 2 else "dealt"
             res_sb[k] = ring.tile([P, 2, S], F32, name="res_sb", tag=tag)
             nc.sync.dma_start(
                 out=res_sb[k][:], in_=res[2 * P * k : 2 * P * (k + 1), :].rearrange("(e p) j -> p e j", p=P)
             )
 
-        fill_page(0)
-        fill_page(1)
-        quantise_w1(1, 0)
-        fill_page(2)
-        quantise_w1(1, 1)
-        quantise_w1(1, 2)
-        fill_page(3)
+        for i in range(2):
+            lay_page(i)
+            put_looks(i)
+        for a in range(KP):
+            quantise_w1(1, a)
+        lay_page(2)
+        lay_page(3)
+        put_looks(2)
+        round_page(0)
+        round_page(1)
         for t in range(PACK):
             for a in range(KP):
                 first_product(PACK + t, a)
-        fill_page(4)
-        fill_page(5)
-        round_page(0)
-        round_page(1)
-        fill_page(6)
+        lay_page(4)
+        put_looks(3)
+        lay_page(5)
+        put_looks(4)
         round_page(2)
+        lay_page(6)
+        put_looks(5)
         round_page(3)
-        fill_page(7)
-        for u in range(HALVES):
-            quantise_z(0, u)
+        lay_page(7)
+        quantise_z(0, 0)
+        put_looks(6)
+        quantise_z(0, 1)
+        put_looks(7)
         for g in range(8):
             second_product(g, 0)
         for i in range(PACK, ROWSETS):
@@ -270,4 +310,10 @@ def tile_list_washed_stroke_fill_kernel(
             second_product(g, 1)
             dst = res_sb[n // 2][:, n % 2, u * BANK : (u + 1) * BANK]
             nc.vector.tensor_tensor(out=dst, in0=outs[g][:], in1=dst, op=ALU.add)
-            nc.sync.dma_start(out=out[n * P : (n + 1) * P, u * BANK : (u + 1) * BANK], in_=dst)
+            if g < 2 or g >= len(groups) - 2:
+                nc.sync.dma_start(out=out[n * P : (n + 1) * P, u * BANK : (u + 1) * BANK], in_=dst)
+            elif n % 2 == 1:
+                nc.sync.dma_start(
+                    out=out[(n - 1) * P : (n + 1) * P, u * BANK : (u + 1) * BANK].rearrange("(e p) j -> p e j", p=P),
+                    in_=res_sb[n // 2][:, :, u * BANK : (u + 1) * BANK],
+                )

@@ -55,8 +55,17 @@ def tile_list_washed_stroke_fill_kernel(
         w4_sc = keep.tile([P, HP, N], U8, name="w4_sc", align_bytes=64)
         nc.vector.memset(w4_sc[:].bitcast(I32), 0)
 
+        vectors = {"b1": b1, "thr": thr, "base": base, "gain": gain}
+
+        def load_rows(names, b):
+            for name in names:
+                rowvec[name, b] = keep.tile([P, PACK], F32, name="row_%s%d" % (name, b))
+                nc.sync.dma_start(
+                    out=rowvec[name, b][:], in_=vectors[name][b * PASS : (b + 1) * PASS].rearrange("(p t) -> p t", t=PACK)
+                )
+
         def col(name, i):
-            return rowvec[name][:, i // PACK, i % PACK : i % PACK + 1]
+            return rowvec[name, i // PACK][:, i % PACK : i % PACK + 1]
 
         tab_sb, raw = {}, {}
 
@@ -87,14 +96,14 @@ def tile_list_washed_stroke_fill_kernel(
         nc.sync.dma_start(pos1_sb[:], pos1)
         nc.sync.dma_start(pos2_sb[:], pos2)
         load_tab(1)
-        for name, vec in (("b1", b1), ("thr", thr), ("base", base), ("gain", gain)):
-            rowvec[name] = keep.tile([P, HP, PACK], F32, name="row_" + name)
-            nc.sync.dma_start(out=rowvec[name][:], in_=vec.rearrange("(b p t) -> p b t", b=HP, t=PACK))
+        load_rows(("b1", "thr", "base"), 0)
         load_w1(0, 1)
         load_tab(2)
         load_w1(0, 2)
         for a in range(KP):
             load_w1(1, a)
+        load_rows(("gain",), 0)
+        load_rows(("b1", "thr", "base", "gain"), 1)
         w4_sb = keep.tile([P, HP, 2 * N], U8, name="w4_sb", align_bytes=64)
         nc.sync.dma_start(out=w4_sb[:].bitcast(I32), in_=w4_words.bitcast(I32).rearrange("a p c -> p a c"))
         for q in range(4):

from contextlib import ExitStack

import concourse.mybir as mybir
from concourse.masks import make_identity

K, H, N, T, S, M = 1536, 1024, 768, 4096, 1024, 512
FLOPS = 2 * K * H * S + 2 * H * N * S

F32 = mybir.dt.float32
BF16 = mybir.dt.bfloat16
I32 = mybir.dt.int32
U32 = mybir.dt.uint32
U16 = mybir.dt.uint16
U8 = mybir.dt.uint8
FP8X4 = mybir.dt.float8_e4m3fn_x4
FP4X4 = mybir.dt.float4_e2m1fn_x4
ACT = mybir.ActivationFunctionType
ALU = mybir.AluOpType

P = 128
PACK = 4
PASS = P * PACK
BANK = 512
KP = K // PASS
HP = H // PASS
HALVES = S // BANK
NT = N // P
ROWSETS = HP * PACK


def tile_list_washed_stroke_fill_kernel(
    tc, tab_words, tab_scales, offs, pos1, pos2, w1, b1, thr, base, wgs, gain, w4_words, w4_scales, res, out
):
    nc = tc.nc
    with ExitStack() as ctx:
        lists = ctx.enter_context(tc.tile_pool(name="lists", bufs=1))
        keep = ctx.enter_context(tc.tile_pool(name="keep", bufs=1))
        ring = ctx.enter_context(tc.tile_pool(name="ring", bufs=1))
        psum = ctx.enter_context(tc.psum_pool(name="psum", bufs=1))

        offs_sb = lists.tile([P, S // 16], U16, name="offs_sb")
        pos1_sb = lists.tile([P, M // 16], U16, name="pos1_sb")
        pos2_sb = lists.tile([P, M // 16], U16, name="pos2_sb")

        ident = keep.tile([P, P], F32, name="ident")
        make_identity(nc, ident[:])
        tab_sc = ring.tile([P, T], U8, name="tab_sc", tag="tab_sc", align_bytes=64)
        nc.vector.memset(tab_sc[:].bitcast(I32), 0)
        for q in range(4):
            nc.gpsimd.dma_start(
                out=tab_sc[32 * q : 32 * q + 4 * KP, :].bitcast(I32),
                in_=tab_scales[:, 4 * q : 4 * q + 4, :].bitcast(I32),
            )
        rowvec = {}
        w4_sc = keep.tile([P, HP, N], U8, name="w4_sc", align_bytes=64)
        nc.vector.memset(w4_sc[:].bitcast(I32), 0)

        vectors = {"b1": b1, "thr": thr, "base": base, "gain": gain}

        def load_rows(names, b):
            for name in names:
                rowvec[name, b] = keep.tile([P, PACK], F32, name="row_%s%d" % (name, b))
                nc.sync.dma_start(
                    out=rowvec[name, b][:], in_=vectors[name][b * PASS : (b + 1) * PASS].rearrange("(p t) -> p t", t=PACK)
                )

        def col(name, i):
            return rowvec[name, i // PACK][:, i % PACK : i % PACK + 1]

        tab_sb, raw = {}, {}

        def load_tab(a):
            tab_sb[a] = keep.tile([P, T], U32, name="tab%d" % a)
            nc.sync.dma_start(
                out=tab_sb[a][:].bitcast(I32), in_=tab_words[a].rearrange("p t i -> p (t i)").bitcast(I32)
            )

        def load_w1(b, a):
            parts = 2 if a == KP - 1 else 1
            width = PASS // parts
            for u in range(parts):
                raw[b, a, u] = ring.tile([P, PACK, width], F32, name="raw%d%d%d" % (b, a, u), tag="raw%d%d%d" % (b, a, u))
                c0 = b * PASS + u * width
                nc.sync.dma_start(
                    out=raw[b, a, u][:],
                    in_=w1[a * PASS : (a + 1) * PASS, c0 : c0 + width].rearrange("(p j) c -> p j c", j=PACK),
                )

        wgs_sb = keep.tile([P, PACK, M], F32, name="wgs_sb")

        nc.sync.dma_start(offs_sb[:], offs)
        wgs_rows = ring.tile([P, M], F32, name="wgs_rows", tag="look", bufs=4)
        nc.sync.dma_start(out=wgs_rows[:], in_=wgs)
        load_tab(0)
        load_w1(0, 0)
        nc.sync.dma_start(pos1_sb[:], pos1)
        nc.sync.dma_start(pos2_sb[:], pos2)
        load_tab(1)
        load_rows(("b1", "thr", "base"), 0)
        load_w1(0, 1)
        load_tab(2)
        load_w1(0, 2)
        for a in range(KP):
            load_w1(1, a)
        load_rows(("gain",), 0)
        load_rows(("b1", "thr", "base", "gain"), 1)
        w4_sb = keep.tile([P, HP, 2 * N], U8, name="w4_sb", align_bytes=64)
        nc.sync.dma_start(out=w4_sb[:].bitcast(I32), in_=w4_words.bitcast(I32).rearrange("a p c -> p a c"))
        for q in range(4):
            nc.sync.dma_start(
                out=w4_sc[32 * q : 32 * q + 4, :, :].bitcast(I32),
                in_=w4_scales[:, 4 * q : 4 * q + 4, :].bitcast(I32).rearrange("a r n -> r a n"),
            )

        v_words = {}
        v_sc = keep.tile([P, S], U8, name="v_sc", align_bytes=64)

        def gather_words(a):
            v_words[a] = keep.tile([P, S], U32, name="v_words%d" % a, align_bytes=64)
            nc.vector.tensor_copy(v_words[a][:], tab_sb[a][:].indirect(offs_sb[:]))

        w1_codes, w1_sc = {}, {}

        def quantise_w1(b, a):
            tag = "tab_sc" if a == 1 else "stage%d" % (a // 2)
            grouped = ring.tile([P, PACK, P, PACK], BF16, name="grouped", tag=tag, align_bytes=64)
            parts = 2 if a == KP - 1 else 1
            mw = P // parts
            for u in range(parts):
                src = raw[b, a, u][:].rearrange("p j (m t) -> p m t j", t=PACK)
                dst = grouped[:, :, u * mw : (u + 1) * mw, :].rearrange("p t m j -> p m t j")
                if u == 0 and (b, a) != (1, 0):
                    nc.scalar.copy(out=dst, in_=src)
                else:
                    nc.vector.tensor_copy(out=dst, in_=src)
            w1_codes[b, a] = keep.tile([P, PASS], U32, name="w1c%d%d" % (b, a), align_bytes=64)
            w1_sc[b, a] = keep.tile([P, PASS], U8, name="w1s%d%d" % (b, a), align_bytes=64)
            flat = grouped[:].rearrange("p t m j -> p (t m j)")
            cuts = (0, P, PASS) if a == KP - 1 else (0, PASS)
            for c0, c1 in zip(cuts, cuts[1:]):
                nc.vector.quantize_mx(
                    out=w1_codes[b, a][:, c0:c1].bitcast(FP8X4),
                    scales=w1_sc[b, a][:, c0:c1],
                    in_=flat[:, PACK * c0 : PACK * c1],
                )

        sums = {}

        def first_product(i, a):
            b, t = divmod(i, PACK)
            for u in range(HALVES):
                if a == 0:
                    sums[i, u] = psum.tile([P, BANK], F32, name="sums", tag="bank%d" % (HALVES * t + u))
                cols = slice(u * BANK, (u + 1) * BANK)
                nc.tensor.matmul_mx(
                    out=sums[i, u][:],
                    lhsT=w1_codes[b, a][:, t * P : (t + 1) * P].bitcast(FP8X4),
                    lhsT_scale=w1_sc[b, a][:, t * P : (t + 1) * P],
                    rhs=v_words[a][:, cols].bitcast(FP8X4),
                    rhs_scale=v_sc[4 * a : P, cols],
                    start=(a == 0),
                    stop=(a == KP - 1),
                )

        page, hs = {}, {}

        def lay_page(i):
            tag = {1: "h0", 2: "raw120"}.get(i, "h%d" % (i % 3))
            h = ring.tile([P, S], F32, name="h", tag=tag)
            for u in range(HALVES):
                cols = slice(u * BANK, (u + 1) * BANK)
                if i == 0:
                    nc.vector.tensor_scalar_add(out=h[:, cols], in0=sums[i, u][:], scalar1=col("b1", i))
                else:
                    nc.scalar.activation(out=h[:, cols], in_=sums[i, u][:], func=ACT.Identity, bias=col("b1", i))
            page[i] = ring.tile([P, S], F32, name="page", tag="page", bufs=6)
            nc.vector.tensor_scalar_max(out=page[i][:], in0=h[:], scalar1=col("base", i))
            hs[i] = h

        def put_looks(i):
            h = hs[i]
            look = ring.tile([P, M], F32, name="look", tag="look", bufs=4)
            parts = 2 if i == 0 else 1
            for e in range(parts):
                ent = slice(e * M // parts, (e + 1) * M // parts)
                lst = slice(e * M // parts // 16, (e + 1) * M // parts // 16)
                nc.scalar.activation(
                    out=look[:, ent], in_=h[:].indirect(pos1_sb[:, lst]), func=ACT.Sigmoid, bias=col("thr", i)
                )
                nc.vector.tensor_tensor(page[i][:].indirect(pos2_sb[:, lst]), look[:, ent], wgs_sb[:, i % PACK, ent], ALU.mult)

        planes = {}

        def round_page(i):
            b, t = divmod(i, PACK)
            if b == 0:
                if t == 0:
                    whole = ring.tile([P, PACK, S], BF16, name="whole", tag="raw120")
                    for u in range(HALVES):
                        planes[b, u] = whole[:, :, u * BANK : (u + 1) * BANK]
                    planes[b] = whole
                nc.scalar.activation(out=planes[b][:, t, :], in_=page[i][:], func=ACT.Copy, scale=col("gain", i))
                return
            for u in range(HALVES):
                if t == 0:
                    planes[b, u] = ring.tile([P, PACK, BANK], BF16, name="planes", tag="planes%d" % u)
                nc.scalar.activation(
                    out=planes[b, u][:, t, :], in_=page[i][:, u * BANK : (u + 1) * BANK], func=ACT.Copy, scale=col("gain", i)
                )

        z_codes, z_sc = {}, {}

        def quantise_z(b, u):
            woven = ring.tile([P, BANK, PACK], BF16, name="woven", tag="woven%d" % u, align_bytes=64)
            z_codes[b, u] = keep.tile([P, BANK], U32, name="zc%d%d" % (b, u), align_bytes=64)
            z_sc[b, u] = keep.tile([P, BANK], U8, name="zs%d%d" % (b, u), align_bytes=64)
            urgent = (b, u) == (HP - 1, 0)
            pieces = [slice(0, BANK // 2), slice(BANK // 2, BANK)] if urgent else [slice(0, BANK)]
            for cols in pieces:
                dst = woven[:, cols, :].rearrange("p (c i) t -> p c t i", i=4)
                src = planes[b, u][:, :, cols].rearrange("p t (c i) -> p c t i", i=4)
                if urgent:
                    nc.vector.tensor_copy(out=dst, in_=src)
                else:
                    nc.scalar.copy(out=dst, in_=src)
            for cols in pieces:
                nc.vector.quantize_mx(
                    out=z_codes[b, u][:, cols].bitcast(FP8X4),
                    scales=z_sc[b, u][:, cols],
                    in_=woven[:, cols, :].rearrange("p c t -> p (c t)"),
                )

        groups = [(u, n) for u in range(HALVES) for n in range(NT)]
        outs = {}

        def second_product(g, b):
            u, n = groups[g]
            if b == 0:
                outs[g] = psum.tile([P, BANK], F32, name="outs", tag="bank%d" % (g % 8))
            pieces = [slice(0, BANK // 2), slice(BANK // 2, BANK)] if (g, b) == (0, HP - 1) else [slice(0, BANK)]
            for cols in pieces:
                nc.tensor.matmul_mx(
                    out=outs[g][:, cols],
                    lhsT=w4_sb[:, b, 2 * P * n : 2 * P * (n + 1)].bitcast(FP4X4),
                    lhsT_scale=w4_sc[:, b, P * n : P * (n + 1)],
                    rhs=z_codes[b, u][:, cols].bitcast(FP8X4),
                    rhs_scale=z_sc[b, u][:, cols],
                    start=(b == 0),
                    stop=(b == HP - 1 and cols.stop == BANK),
                )

        turned = psum.tile([P, M // P, P], F32, name="turned", tag="bank0")
        for k in range(M // P):
            nc.tensor.transpose(turned[:, k, :], wgs_rows[:, k * P : (k + 1) * P], ident[:])
        dealt = ring.tile([P, M // P, PACK, P], F32, name="dealt", tag="dealt")
        for c in range(4):
            nc.vector.tensor_copy(out=dealt[:, :, :, 32 * c : 32 * (c + 1)], in_=turned[:].rearrange("m k (q t) -> m k t q", t=PACK))
        for t in range(PACK):
            back = psum.tile([P, M // P, P], F32, name="back", tag="bank%d" % (1 + t))
            for k in range(M // P):
                nc.tensor.transpose(back[:, k, :], dealt[:, k, t, :], ident[:])
            nc.scalar.copy(out=wgs_sb[:, t, :], in_=back[:].rearrange("p k m -> p (k m)"))

        gather_words(0)
        quantise_w1(0, 0)
        nc.vector.tensor_copy(v_sc[:], tab_sc[:].indirect(offs_sb[:]))
        for a in range(KP):
            if a > 0:
                gather_words(a)
                quantise_w1(0, a)
            for t in range(PACK):
                first_product(t, a)

        res_sb = {}
        for k in range(NT // 2):
            tag = "raw0%d0" % k if k < 2 else "dealt"
            res_sb[k] = ring.tile([P, 2, S], F32, name="res_sb", tag=tag)
            nc.sync.dma_start(
                out=res_sb[k][:], in_=res[2 * P * k : 2 * P * (k + 1), :].rearrange("(e p) j -> p e j", p=P)
            )

        for i in range(2):
            lay_page(i)
            put_looks(i)
        for a in range(KP):
            quantise_w1(1, a)
        lay_page(2)
        lay_page(3)
        put_looks(2)
        round_page(0)
        round_page(1)
        for t in range(PACK):
            for a in range(KP):
                first_product(PACK + t, a)
        lay_page(4)
        put_looks(3)
        lay_page(5)
        put_looks(4)
        round_page(2)
        lay_page(6)
        put_looks(5)
        round_page(3)
        lay_page(7)
        quantise_z(0, 0)
        put_looks(6)
        quantise_z(0, 1)
        put_looks(7)
        for g in range(8):
            second_product(g, 0)
        for i in range(PACK, ROWSETS):
            round_page(i)

        for u in range(HALVES):
            quantise_z(1, u)
        for g in range(len(groups)):
            u, n = groups[g]
            if g >= 8:
                second_product(g, 0)
            second_product(g, 1)
            dst = res_sb[n // 2][:, n % 2, u * BANK : (u + 1) * BANK]
            nc.vector.tensor_tensor(out=dst, in0=outs[g][:], in1=dst, op=ALU.add)
            if g < 2 or g >= len(groups) - 2:
                nc.sync.dma_start(out=out[n * P : (n + 1) * P, u * BANK : (u + 1) * BANK], in_=dst)
            elif n % 2 == 1:
                nc.sync.dma_start(
                    out=out[(n - 1) * P : (n + 1) * P, u * BANK : (u + 1) * BANK].rearrange("(e p) j -> p e j", p=P),
                    in_=res_sb[n // 2][:, :, u * BANK : (u + 1) * BANK],
                )
